import numpy as np
import ml_dtypes


def mxq(x, axis, fmt="e4m3"):
    dtype, down = {"e4m3": (ml_dtypes.float8_e4m3fn, 7), "e5m2": (ml_dtypes.float8_e5m2, 14)}[fmt]
    v = np.moveaxis(np.asarray(x, np.float32).astype(ml_dtypes.bfloat16).astype(np.float64), axis, -1)
    blocks = v.reshape(v.shape[:-1] + (-1, 32))
    amax = np.abs(blocks).max(-1, keepdims=True)
    byte = np.maximum(np.where(amax > 0, np.frexp(amax)[1] - 1 + 127, 0) - down, 1)
    scale = np.exp2(byte - 127.0)
    codes = (blocks / scale).astype(np.float32).astype(dtype).astype(np.float64)
    return np.moveaxis((codes * scale).reshape(v.shape), -1, axis)


WIDE = False


def mx_kscale(k):
    if not WIDE:
        return np.ones(k)
    levels = np.array([10, -10, 5, -5, 0])
    if k % 512:
        return np.exp2(np.random.permutation(np.resize(levels, k // 32))).repeat(32)
    a = np.empty((k // 512, 16))
    for p in range(k // 512):
        a[p, :8] = np.random.permutation(np.resize(levels, 8))
        for g in range(8):
            far = levels[np.abs(levels - a[p, g]) >= 10]
            a[p, g + 8] = far[np.random.randint(len(far))]
    return np.exp2(a.ravel()).repeat(32)


def f64(x):
    return np.asarray(x).astype(np.float64)


E2M1 = np.array([0.0, 0.5, 1.0, 1.5, 2.0, 3.0, 4.0, 6.0, -0.0, -0.5, -1.0, -1.5, -2.0, -3.0, -4.0, -6.0])


def pack_weight(w, fmt):
    k, n = w.shape
    w = f64(np.asarray(w, np.float32).astype(ml_dtypes.bfloat16)).reshape(k // 32, 32, n)
    amax = np.abs(w).max(1)
    if fmt == "e4m3":
        byte = np.frexp(amax)[1] - 1 + 127 - 7
    else:
        mant, ex = np.frexp(amax / 6.0)
        byte = np.where(mant > 0.5, ex, ex - 1) + 127
    byte = np.clip(np.where(amax > 0, byte, 1), 1, 254)
    scaled = (w * np.exp2(127.0 - byte)[:, None, :]).reshape(k, n).astype(np.float32)
    by_word = np.ascontiguousarray(scaled.reshape(k // 512, 128, 4, n).transpose(0, 1, 3, 2))
    if fmt == "e4m3":
        words = by_word.astype(ml_dtypes.float8_e4m3fn).view(np.uint8)
    else:
        c = by_word.astype(ml_dtypes.float4_e2m1fn).view(np.uint8) & 0xF
        words = (c[..., 0::2] | (c[..., 1::2] << 4)).reshape(k // 512, 128, 2 * n)
    return np.ascontiguousarray(words), np.ascontiguousarray(byte.astype(np.uint8).reshape(k // 512, 16, n))


def unpack_weight(words, scales, fmt):
    g, _, n = scales.shape
    words = np.ascontiguousarray(words).reshape(g, 128, n, -1)
    if fmt == "e4m3":
        vals = words.view(ml_dtypes.float8_e4m3fn).astype(np.float64)
    else:
        nib = np.empty((g, 128, n, 4), np.uint8)
        nib[..., 0::2] = words & 0xF
        nib[..., 1::2] = words >> 4
        vals = E2M1[nib]
    vals = vals * np.repeat(np.exp2(scales.astype(np.float64) - 127.0), 8, axis=1)[..., None]
    return vals.transpose(0, 1, 3, 2).reshape(g * 512, n)


K, M, T = 512, 1024, 1024


def setup_inputs():
    n = np.random.standard_normal
    s = mx_kscale(K)[:, None]
    u = mx_kscale(T)[:, None]
    q = n((K, T)) * s
    p_vc = pack_weight(0.1 * n((T, M)) / u, "e2m1")
    return {
        "qc": (q).astype(np.float32),
        "kc": (n((K, T)) / np.sqrt(K) / s).astype(np.float32),
        "qd": (q * 0.995 ** (np.arange(T) + 1.0)).astype(np.float32),
        "st": (n((K, M)) / np.sqrt(K) / s).astype(np.float32),
        "vc_words": p_vc[0],
        "vc_scales": p_vc[1],
        "dm": (np.tril(0.995 ** (np.arange(T)[:, None] - np.arange(T)[None])).T * u).astype(np.float32),
    }


def reference(qc, kc, qd, st, vc_words, vc_scales, dm):
    qc_ = mxq(f64(qc), 0, "e4m3")
    kc_ = mxq(f64(kc), 0, "e4m3")
    qd_ = mxq(f64(qd), 0, "e4m3")
    st_ = mxq(f64(st), 0, "e4m3")
    vc_ = unpack_weight(vc_words, vc_scales, "e2m1")
    h_ = mxq((kc_.T @ qc_) * f64(dm), 0, "e4m3")
    y = h_.T @ vc_ + qd_.T @ st_
    return y

@@ -1,0 +1,214 @@
+from contextlib import ExitStack
+
+import concourse.mybir as mybir
+
+K, M, T = 512, 1024, 1024
+FLOPS = 2 * K * T * T // 2 + 2 * T * T * M // 2 + 2 * K * T * M
+BYTES = 4 * (4 * K * T + T * T // 2 + T * M) + T * M // 2 + T * M // 32
+
+F32 = mybir.dt.float32
+BF16 = mybir.dt.bfloat16
+I32 = mybir.dt.int32
+U32 = mybir.dt.uint32
+U8 = mybir.dt.uint8
+FP8X4 = mybir.dt.float8_e4m3fn_x4
+FP4X4 = mybir.dt.float4_e2m1fn_x4
+MULT = mybir.AluOpType.mult
+
+P = 128
+PACK = 4
+HALF = 512
+TILE = 128
+
+
+def tile_mix_linattn_tm_none_kernel(tc, qc, kc, qd, st, vc_words, vc_scales, dm, out):
+    nc = tc.nc
+
+    with ExitStack() as ctx:
+        sb = ctx.enter_context(tc.tile_pool(name="sb", bufs=1))
+        score_pool = ctx.enter_context(tc.psum_pool(name="scores", bufs=2))
+        sum_pool = ctx.enter_context(tc.psum_pool(name="sums", bufs=6))
+        ctx.enter_context(tc.manual_schedule())
+
+        def load(name, rows):
+            raw = sb.tile([P, PACK, HALF], F32, name=name, align_bytes=64)
+            nc.sync.dma_start(out=raw[:], in_=rows.rearrange("(p e) w -> p e w", e=PACK))
+            return raw
+
+        def operand(name):
+            staged = sb.tile([P, HALF * PACK], BF16, name=name + "_bf", align_bytes=64)
+            codes = sb.tile([P, HALF], U32, name=name + "_codes", align_bytes=64)
+            scales = sb.tile([P, HALF], U8, name=name + "_scales", align_bytes=64)
+            return staged, codes, scales
+
+        def copy_on(engine, dst, src):
+            if engine == "vector":
+                nc.vector.tensor_copy(out=dst, in_=src)
+            else:
+                nc.scalar.copy(out=dst, in_=src)
+
+        def interleave(engine, raw, op, c0, c1):
+            dst = op[0][:, PACK * c0 : PACK * c1].rearrange("p (c u e) -> p c e u", u=2, e=PACK)
+            src = raw[:, :, c0:c1].rearrange("p e (c u) -> p c e u", u=2)
+            copy_on(engine, dst, src)
+
+        def interleave_keys(engine, raw, op, i0):
+            dst = op[0][:].rearrange("p (i m e) -> p m e i", i=PACK, e=PACK)[:, :, :, i0 : i0 + 2]
+            src = raw[:].rearrange("p e (m i) -> p m e i", i=PACK)[:, :, :, i0 : i0 + 2]
+            copy_on(engine, dst, src)
+
+        def quantize(op, c0, c1):
+            nc.vector.quantize_mx(
+                out=op[1][:, c0:c1].bitcast(FP8X4), scales=op[2][:, c0:c1], in_=op[0][:, PACK * c0 : PACK * c1]
+            )
+
+        def prepare_on_vector(raw, op):
+            interleave("vector", raw, op, 0, 256)
+            interleave("vector", raw, op, 256, 512)
+            quantize(op, 0, 256)
+            quantize(op, 256, 512)
+
+        def weigh_tile(keys, queries, decay, h, n):
+            cols = slice(n * TILE, (n + 1) * TILE)
+            bank = score_pool.tile([P, PACK, TILE], F32, name="score_bank")
+            for i in range(PACK):
+                key_cols = slice(i * TILE, (i + 1) * TILE)
+                nc.tensor.matmul_mx(
+                    out=bank[:, i, :],
+                    lhsT=keys[1][:, key_cols].bitcast(FP8X4),
+                    lhsT_scale=keys[2][:, key_cols],
+                    rhs=queries[1][:, cols].bitcast(FP8X4),
+                    rhs_scale=queries[2][:, cols],
+                    start=True,
+                    stop=True,
+                )
+            nc.vector.tensor_tensor(
+                out=h[0][:, PACK * n * TILE : PACK * (n + 1) * TILE].rearrange("p (c u i) -> p c i u", u=2, i=PACK),
+                in0=bank[:].rearrange("p i (c u) -> p c i u", u=2),
+                in1=decay[:, :, cols].rearrange("p i (c u) -> p c i u", u=2),
+                op=MULT,
+            )
+
+        def weigh(keys, queries, decay, h):
+            for n in range(4):
+                weigh_tile(keys, queries, decay, h, n)
+                if n > 0:
+                    quantize(h, (n - 1) * TILE, n * TILE)
+
+        lo, hi = slice(0, HALF), slice(HALF, T)
+        v_scales = sb.tile([P, 2, M], U8, name="v_scales", align_bytes=64)
+        nc.vector.memset(v_scales[:].rearrange("p a n -> p (a n)").bitcast(I32), 0)
+        kc_lo_raw = load("kc_lo_raw", kc[:, lo])
+        qc_hi_raw = load("qc_hi_raw", qc[:, hi])
+        for q in range(4):
+            nc.scalar.dma_start(
+                out=v_scales[32 * q : 32 * q + 4, :, :].bitcast(I32),
+                in_=vc_scales[:, 4 * q : 4 * q + 4, :].rearrange("a r n -> r a n").bitcast(I32),
+            )
+        dm_lo_hi = load("dm_lo_hi", dm[lo, hi])
+        kc_hi_raw = load("kc_hi_raw", kc[:, hi])
+        dm_hi_hi = load("dm_hi_hi", dm[hi, hi])
+        v_words = sb.tile([P, 2, 2 * M], U8, name="v_words", align_bytes=64)
+        nc.sync.dma_start(out=v_words[:].bitcast(I32), in_=vc_words.rearrange("a p b -> p a b").bitcast(I32))
+        st_lo_raw = load("st_lo_raw", st[:, lo])
+        qd_hi_raw = load("qd_hi_raw", qd[:, hi])
+        st_hi_raw = load("st_hi_raw", st[:, hi])
+        qc_lo_raw = load("qc_lo_raw", qc[:, lo])
+        dm_lo_lo = load("dm_lo_lo", dm[lo, lo])
+        qd_lo_raw = load("qd_lo_raw", qd[:, lo])
+
+        kc_lo, kc_hi = operand("kc_lo"), operand("kc_hi")
+        qc_lo, qc_hi = operand("qc_lo"), operand("qc_hi")
+        qd_lo, qd_hi = operand("qd_lo"), operand("qd_hi")
+        st_half = [operand("st_lo"), operand("st_hi")]
+        h_lo_hi, h_hi_hi, h_lo_lo = operand("h_lo_hi"), operand("h_hi_hi"), operand("h_lo_lo")
+        results = [sb.tile([P, M], F32, name="result%d" % n, align_bytes=64) for n in range(8)]
+        sums = {}
+
+        def value_pass(tile, half, h, a, start):
+            if start:
+                sums[(tile, half)] = sum_pool.tile([P, HALF], F32, name="sum_bank")
+            cols = slice((tile % 4) * TILE, (tile % 4 + 1) * TILE)
+            nc.tensor.matmul_mx(
+                out=sums[(tile, half)][:],
+                lhsT=h[1][:, cols].bitcast(FP8X4),
+                lhsT_scale=h[2][:, cols],
+                rhs=v_words[:, a, 2 * half * HALF : 2 * (half + 1) * HALF].bitcast(FP4X4),
+                rhs_scale=v_scales[:, a, half * HALF : (half + 1) * HALF],
+                start=start,
+                stop=False,
+            )
+
+        def state_pass(tile, half, queries):
+            cols = slice((tile % 4) * TILE, (tile % 4 + 1) * TILE)
+            nc.tensor.matmul_mx(
+                out=sums[(tile, half)][:],
+                lhsT=queries[1][:, cols].bitcast(FP8X4),
+                lhsT_scale=queries[2][:, cols],
+                rhs=st_half[half][1][:].bitcast(FP8X4),
+                rhs_scale=st_half[half][2][:],
+                start=False,
+                stop=True,
+            )
+
+        def drain(engine, tile, half):
+            copy_on(engine, results[tile][:, half * HALF : (half + 1) * HALF], sums[(tile, half)][:])
+
+        def store(tile):
+            nc.sync.dma_start(out=out[tile * TILE : (tile + 1) * TILE, :], in_=results[tile][:])
+
+        interleave_keys("vector", kc_lo_raw, kc_lo, 0)
+        interleave_keys("vector", kc_lo_raw, kc_lo, 2)
+        quantize(kc_lo, 0, 256)
+        quantize(kc_lo, 256, 512)
+        prepare_on_vector(qc_hi_raw, qc_hi)
+        weigh(kc_lo, qc_hi, dm_lo_hi, h_lo_hi)
+        interleave_keys("scalar", kc_hi_raw, kc_hi, 0)
+        interleave_keys("scalar", kc_hi_raw, kc_hi, 2)
+        quantize(kc_hi, 0, 256)
+        quantize(h_lo_hi, 3 * TILE, 4 * TILE)
+        quantize(kc_hi, 256, 512)
+        weigh(kc_hi, qc_hi, dm_hi_hi, h_hi_hi)
+        interleave("scalar", st_lo_raw, st_half[0], 0, 256)
+        interleave("scalar", st_lo_raw, st_half[0], 256, 512)
+        quantize(st_half[0], 0, 256)
+        quantize(h_hi_hi, 3 * TILE, 4 * TILE)
+        for tile, half in [(4, 0), (5, 0), (6, 0), (7, 0), (4, 1), (5, 1)]:
+            value_pass(tile, half, h_lo_hi, 0, True)
+            value_pass(tile, half, h_hi_hi, 1, False)
+        interleave("vector", qd_hi_raw, qd_hi, 0, 256)
+        quantize(st_half[0], 256, 512)
+        interleave("vector", qd_hi_raw, qd_hi, 256, 512)
+        quantize(qd_hi, 0, 256)
+        quantize(qd_hi, 256, 512)
+        for tile in range(4, 8):
+            state_pass(tile, 0, qd_hi)
+            drain("scalar", tile, 0)
+        for tile in (6, 7):
+            value_pass(tile, 1, h_lo_hi, 0, True)
+            value_pass(tile, 1, h_hi_hi, 1, False)
+        prepare_on_vector(st_hi_raw, st_half[1])
+        for tile in range(4, 8):
+            state_pass(tile, 1, qd_hi)
+            drain("scalar", tile, 1)
+            store(tile)
+
+        prepare_on_vector(qc_lo_raw, qc_lo)
+        weigh(kc_lo, qc_lo, dm_lo_lo, h_lo_lo)
+        for tile in range(3):
+            value_pass(tile, 0, h_lo_lo, 0, True)
+            value_pass(tile, 1, h_lo_lo, 0, True)
+        interleave("scalar", qd_lo_raw, qd_lo, 0, 256)
+        interleave("vector", qd_lo_raw, qd_lo, 256, 512)
+        quantize(h_lo_lo, 3 * TILE, 4 * TILE)
+        quantize(qd_lo, 0, 256)
+        quantize(qd_lo, 256, 512)
+        for tile in range(4):
+            if tile == 3:
+                value_pass(tile, 0, h_lo_lo, 0, True)
+                value_pass(tile, 1, h_lo_lo, 0, True)
+            state_pass(tile, 0, qd_lo)
+            state_pass(tile, 1, qd_lo)
+            drain("scalar", tile, 0)
+            drain("vector", tile, 1)
+            store(tile)

@@ -31,7 +31,7 @@ def tile_mix_linattn_tm_none_kernel(tc, qc, kc, qd, st, vc_words, vc_scales, dm,
         ctx.enter_context(tc.manual_schedule())
 
         def load(name, rows):
-            raw = sb.tile([P, PACK, HALF], F32, name=name, align_bytes=64)
+            raw = sb.tile([P, PACK, rows.shape[1]], F32, name=name, align_bytes=64)
             nc.sync.dma_start(out=raw[:], in_=rows.rearrange("(p e) w -> p e w", e=PACK))
             return raw
 
@@ -54,7 +54,7 @@ def tile_mix_linattn_tm_none_kernel(tc, qc, kc, qd, st, vc_words, vc_scales, dm,
 
         def interleave_keys(engine, raw, op, i0):
             dst = op[0][:].rearrange("p (i m e) -> p m e i", i=PACK, e=PACK)[:, :, :, i0 : i0 + 2]
-            src = raw[:].rearrange("p e (m i) -> p m e i", i=PACK)[:, :, :, i0 : i0 + 2]
+            src = raw.rearrange("p e (m i) -> p m e i", i=PACK)[:, :, :, i0 : i0 + 2]
             copy_on(engine, dst, src)
 
         def quantize(op, c0, c1):
@@ -62,11 +62,16 @@ def tile_mix_linattn_tm_none_kernel(tc, qc, kc, qd, st, vc_words, vc_scales, dm,
                 out=op[1][:, c0:c1].bitcast(FP8X4), scales=op[2][:, c0:c1], in_=op[0][:, PACK * c0 : PACK * c1]
             )
 
-        def prepare_on_vector(raw, op):
-            interleave("vector", raw, op, 0, 256)
-            interleave("vector", raw, op, 256, 512)
-            quantize(op, 0, 256)
-            quantize(op, 256, 512)
+        def prepare_pair(on_vector, on_scalar, is_keys):
+            for engine, (raw, op) in (("vector", on_vector), ("scalar", on_scalar)):
+                for part in range(2):
+                    if is_keys:
+                        interleave_keys(engine, raw, op, 2 * part)
+                    else:
+                        interleave(engine, raw, op, 256 * part, 256 * (part + 1))
+            for (raw, op) in (on_vector, on_scalar):
+                quantize(op, 0, 256)
+                quantize(op, 256, 512)
 
         def weigh_tile(keys, queries, decay, h, n):
             cols = slice(n * TILE, (n + 1) * TILE)
@@ -89,33 +94,23 @@ def tile_mix_linattn_tm_none_kernel(tc, qc, kc, qd, st, vc_words, vc_scales, dm,
                 op=MULT,
             )
 
-        def weigh(keys, queries, decay, h):
-            for n in range(4):
-                weigh_tile(keys, queries, decay, h, n)
-                if n > 0:
-                    quantize(h, (n - 1) * TILE, n * TILE)
-
         lo, hi = slice(0, HALF), slice(HALF, T)
         v_scales = sb.tile([P, 2, M], U8, name="v_scales", align_bytes=64)
         nc.vector.memset(v_scales[:].rearrange("p a n -> p (a n)").bitcast(I32), 0)
-        kc_lo_raw = load("kc_lo_raw", kc[:, lo])
-        qc_hi_raw = load("qc_hi_raw", qc[:, hi])
+        kc_raw = load("kc_raw", kc)
+        qc_raw = load("qc_raw", qc)
         for q in range(4):
             nc.scalar.dma_start(
                 out=v_scales[32 * q : 32 * q + 4, :, :].bitcast(I32),
                 in_=vc_scales[:, 4 * q : 4 * q + 4, :].rearrange("a r n -> r a n").bitcast(I32),
             )
-        dm_lo_hi = load("dm_lo_hi", dm[lo, hi])
-        kc_hi_raw = load("kc_hi_raw", kc[:, hi])
-        dm_hi_hi = load("dm_hi_hi", dm[hi, hi])
+        dm_lo = load("dm_lo", dm[lo, :])
         v_words = sb.tile([P, 2, 2 * M], U8, name="v_words", align_bytes=64)
         nc.sync.dma_start(out=v_words[:].bitcast(I32), in_=vc_words.rearrange("a p b -> p a b").bitcast(I32))
-        st_lo_raw = load("st_lo_raw", st[:, lo])
-        qd_hi_raw = load("qd_hi_raw", qd[:, hi])
-        st_hi_raw = load("st_hi_raw", st[:, hi])
-        qc_lo_raw = load("qc_lo_raw", qc[:, lo])
-        dm_lo_lo = load("dm_lo_lo", dm[lo, lo])
+        st_raw = load("st_raw", st)
         qd_lo_raw = load("qd_lo_raw", qd[:, lo])
+        dm_hi_hi = load("dm_hi_hi", dm[hi, hi])
+        qd_hi_raw = load("qd_hi_raw", qd[:, hi])
 
         kc_lo, kc_hi = operand("kc_lo"), operand("kc_hi")
         qc_lo, qc_hi = operand("qc_lo"), operand("qc_hi")
@@ -125,90 +120,91 @@ def tile_mix_linattn_tm_none_kernel(tc, qc, kc, qd, st, vc_words, vc_scales, dm,
         results = [sb.tile([P, M], F32, name="result%d" % n, align_bytes=64) for n in range(8)]
         sums = {}
 
-        def value_pass(tile, half, h, a, start):
-            if start:
-                sums[(tile, half)] = sum_pool.tile([P, HALF], F32, name="sum_bank")
+        def value_passes(tile, h, a):
             cols = slice((tile % 4) * TILE, (tile % 4 + 1) * TILE)
-            nc.tensor.matmul_mx(
-                out=sums[(tile, half)][:],
-                lhsT=h[1][:, cols].bitcast(FP8X4),
-                lhsT_scale=h[2][:, cols],
-                rhs=v_words[:, a, 2 * half * HALF : 2 * (half + 1) * HALF].bitcast(FP4X4),
-                rhs_scale=v_scales[:, a, half * HALF : (half + 1) * HALF],
-                start=start,
-                stop=False,
-            )
+            for half in range(2):
+                if a == 0:
+                    sums[(tile, half)] = sum_pool.tile([P, HALF], F32, name="sum_bank")
+                nc.tensor.matmul_mx(
+                    out=sums[(tile, half)][:],
+                    lhsT=h[1][:, cols].bitcast(FP8X4),
+                    lhsT_scale=h[2][:, cols],
+                    rhs=v_words[:, a, 2 * half * HALF : 2 * (half + 1) * HALF].bitcast(FP4X4),
+                    rhs_scale=v_scales[:, a, half * HALF : (half + 1) * HALF],
+                    start=(a == 0),
+                    stop=False,
+                )
 
-        def state_pass(tile, half, queries):
+        def state_passes(tile, queries):
             cols = slice((tile % 4) * TILE, (tile % 4 + 1) * TILE)
-            nc.tensor.matmul_mx(
-                out=sums[(tile, half)][:],
-                lhsT=queries[1][:, cols].bitcast(FP8X4),
-                lhsT_scale=queries[2][:, cols],
-                rhs=st_half[half][1][:].bitcast(FP8X4),
-                rhs_scale=st_half[half][2][:],
-                start=False,
-                stop=True,
-            )
+            for half in range(2):
+                nc.tensor.matmul_mx(
+                    out=sums[(tile, half)][:],
+                    lhsT=queries[1][:, cols].bitcast(FP8X4),
+                    lhsT_scale=queries[2][:, cols],
+                    rhs=st_half[half][1][:].bitcast(FP8X4),
+                    rhs_scale=st_half[half][2][:],
+                    start=False,
+                    stop=True,
+                )
 
-        def drain(engine, tile, half):
-            copy_on(engine, results[tile][:, half * HALF : (half + 1) * HALF], sums[(tile, half)][:])
-
-        def store(tile):
+        def finish(tile, engines):
+            for half in range(2):
+                copy_on(engines[half], results[tile][:, half * HALF : (half + 1) * HALF], sums[(tile, half)][:])
             nc.sync.dma_start(out=out[tile * TILE : (tile + 1) * TILE, :], in_=results[tile][:])
 
-        interleave_keys("vector", kc_lo_raw, kc_lo, 0)
-        interleave_keys("vector", kc_lo_raw, kc_lo, 2)
-        quantize(kc_lo, 0, 256)
-        quantize(kc_lo, 256, 512)
-        prepare_on_vector(qc_hi_raw, qc_hi)
-        weigh(kc_lo, qc_hi, dm_lo_hi, h_lo_hi)
-        interleave_keys("scalar", kc_hi_raw, kc_hi, 0)
-        interleave_keys("scalar", kc_hi_raw, kc_hi, 2)
-        quantize(kc_hi, 0, 256)
-        quantize(h_lo_hi, 3 * TILE, 4 * TILE)
-        quantize(kc_hi, 256, 512)
-        weigh(kc_hi, qc_hi, dm_hi_hi, h_hi_hi)
-        interleave("scalar", st_lo_raw, st_half[0], 0, 256)
-        interleave("scalar", st_lo_raw, st_half[0], 256, 512)
-        quantize(st_half[0], 0, 256)
-        quantize(h_hi_hi, 3 * TILE, 4 * TILE)
-        for tile, half in [(4, 0), (5, 0), (6, 0), (7, 0), (4, 1), (5, 1)]:
-            value_pass(tile, half, h_lo_hi, 0, True)
-            value_pass(tile, half, h_hi_hi, 1, False)
-        interleave("vector", qd_hi_raw, qd_hi, 0, 256)
-        quantize(st_half[0], 256, 512)
-        interleave("vector", qd_hi_raw, qd_hi, 256, 512)
-        quantize(qd_hi, 0, 256)
-        quantize(qd_hi, 256, 512)
-        for tile in range(4, 8):
-            state_pass(tile, 0, qd_hi)
-            drain("scalar", tile, 0)
-        for tile in (6, 7):
-            value_pass(tile, 1, h_lo_hi, 0, True)
-            value_pass(tile, 1, h_hi_hi, 1, False)
-        prepare_on_vector(st_hi_raw, st_half[1])
-        for tile in range(4, 8):
-            state_pass(tile, 1, qd_hi)
-            drain("scalar", tile, 1)
-            store(tile)
+        prepare_pair((kc_raw[:, :, lo], kc_lo), (kc_raw[:, :, hi], kc_hi), True)
+        prepare_pair((qc_raw[:, :, lo], qc_lo), (qc_raw[:, :, hi], qc_hi), False)
 
-        prepare_on_vector(qc_lo_raw, qc_lo)
-        weigh(kc_lo, qc_lo, dm_lo_lo, h_lo_lo)
+        steps = [(qc_lo, dm_lo[:, :, lo], h_lo_lo, n) for n in range(4)]
+        steps = steps + [(qc_hi, dm_lo[:, :, hi], h_lo_hi, n) for n in range(4)]
+        for s, (queries, decay, h, n) in enumerate(steps):
+            weigh_tile(kc_lo, queries, decay, h, n)
+            if s > 0:
+                quantize(steps[s - 1][2], steps[s - 1][3] * TILE, (steps[s - 1][3] + 1) * TILE)
         for tile in range(3):
-            value_pass(tile, 0, h_lo_lo, 0, True)
-            value_pass(tile, 1, h_lo_lo, 0, True)
-        interleave("scalar", qd_lo_raw, qd_lo, 0, 256)
+            value_passes(tile, h_lo_lo, 0)
+
+        interleave("vector", st_raw[:, :, lo], st_half[0], 0, 256)
+        quantize(h_lo_hi, 3 * TILE, 4 * TILE)
+        interleave("vector", st_raw[:, :, lo], st_half[0], 256, 512)
+        interleave("scalar", st_raw[:, :, hi], st_half[1], 0, 256)
+        interleave("scalar", st_raw[:, :, hi], st_half[1], 256, 512)
+        for half in range(2):
+            quantize(st_half[half], 0, 256)
+            quantize(st_half[half], 256, 512)
+
+        interleave("vector", qd_lo_raw, qd_lo, 0, 256)
         interleave("vector", qd_lo_raw, qd_lo, 256, 512)
-        quantize(h_lo_lo, 3 * TILE, 4 * TILE)
         quantize(qd_lo, 0, 256)
         quantize(qd_lo, 256, 512)
-        for tile in range(4):
-            if tile == 3:
-                value_pass(tile, 0, h_lo_lo, 0, True)
-                value_pass(tile, 1, h_lo_lo, 0, True)
-            state_pass(tile, 0, qd_lo)
-            state_pass(tile, 1, qd_lo)
-            drain("scalar", tile, 0)
-            drain("vector", tile, 1)
-            store(tile)
+        for tile in range(3):
+            state_passes(tile, qd_lo)
+            finish(tile, ("scalar", "scalar"))
+        value_passes(3, h_lo_lo, 0)
+        state_passes(3, qd_lo)
+
+        weigh_tile(kc_hi, qc_hi, dm_hi_hi, h_hi_hi, 0)
+        weigh_tile(kc_hi, qc_hi, dm_hi_hi, h_hi_hi, 1)
+        quantize(h_hi_hi, 0, TILE)
+        value_passes(4, h_lo_hi, 0)
+        finish(3, ("scalar", "scalar"))
+        weigh_tile(kc_hi, qc_hi, dm_hi_hi, h_hi_hi, 2)
+        quantize(h_hi_hi, TILE, 2 * TILE)
+        value_passes(5, h_lo_hi, 0)
+        weigh_tile(kc_hi, qc_hi, dm_hi_hi, h_hi_hi, 3)
+        quantize(h_hi_hi, 2 * TILE, 3 * TILE)
+        value_passes(6, h_lo_hi, 0)
+        interleave("scalar", qd_hi_raw, qd_hi, 0, 256)
+        interleave("vector", qd_hi_raw, qd_hi, 256, 512)
+        quantize(h_hi_hi, 3 * TILE, 4 * TILE)
+        quantize(qd_hi, 0, 256)
+        quantize(qd_hi, 256, 512)
+        for tile in range(4, 7):
+            value_passes(tile, h_hi_hi, 1)
+        for tile in range(4, 8):
+            if tile == 7:
+                value_passes(tile, h_lo_hi, 0)
+                value_passes(tile, h_hi_hi, 1)
+            state_passes(tile, qd_hi)
+            finish(tile, ("scalar", "vector"))

@@ -26,8 +26,7 @@ def tile_mix_linattn_tm_none_kernel(tc, qc, kc, qd, st, vc_words, vc_scales, dm,
 
     with ExitStack() as ctx:
         sb = ctx.enter_context(tc.tile_pool(name="sb", bufs=1))
-        score_pool = ctx.enter_context(tc.psum_pool(name="scores", bufs=2))
-        sum_pool = ctx.enter_context(tc.psum_pool(name="sums", bufs=6))
+        psum = ctx.enter_context(tc.psum_pool(name="psum", bufs=8))
         ctx.enter_context(tc.manual_schedule())
 
         def load(name, rows):
@@ -73,13 +72,13 @@ def tile_mix_linattn_tm_none_kernel(tc, qc, kc, qd, st, vc_words, vc_scales, dm,
                 quantize(op, 0, 256)
                 quantize(op, 256, 512)
 
-        def weigh_tile(keys, queries, decay, h, n):
+        def scores(keys, queries, n):
             cols = slice(n * TILE, (n + 1) * TILE)
-            bank = score_pool.tile([P, PACK, TILE], F32, name="score_bank")
+            bank = psum.tile([P, HALF], F32, name="bank")
             for i in range(PACK):
                 key_cols = slice(i * TILE, (i + 1) * TILE)
                 nc.tensor.matmul_mx(
-                    out=bank[:, i, :],
+                    out=bank[:, key_cols],
                     lhsT=keys[1][:, key_cols].bitcast(FP8X4),
                     lhsT_scale=keys[2][:, key_cols],
                     rhs=queries[1][:, cols].bitcast(FP8X4),
@@ -87,12 +86,24 @@ def tile_mix_linattn_tm_none_kernel(tc, qc, kc, qd, st, vc_words, vc_scales, dm,
                     start=True,
                     stop=True,
                 )
+            return bank
+
+        def parked_scores(engine, keys, queries, n, name):
+            bank = scores(keys, queries, n)
+            parked = sb.tile([P, HALF], F32, name=name, align_bytes=64)
+            copy_on(engine, parked[:], bank[:])
+            return parked
+
+        def weigh(raw_scores, decay, d, h, n):
             nc.vector.tensor_tensor(
                 out=h[0][:, PACK * n * TILE : PACK * (n + 1) * TILE].rearrange("p (c u i) -> p c i u", u=2, i=PACK),
-                in0=bank[:].rearrange("p i (c u) -> p c i u", u=2),
-                in1=decay[:, :, cols].rearrange("p i (c u) -> p c i u", u=2),
+                in0=raw_scores[:].rearrange("p (i c u) -> p c i u", u=2, i=PACK),
+                in1=decay[:, :, d * TILE : (d + 1) * TILE].rearrange("p i (c u) -> p c i u", u=2),
                 op=MULT,
             )
+
+        def quantize_tile(op, n):
+            quantize(op, n * TILE, (n + 1) * TILE)
 
         lo, hi = slice(0, HALF), slice(HALF, T)
         v_scales = sb.tile([P, 2, M], U8, name="v_scales", align_bytes=64)
@@ -104,13 +115,15 @@ def tile_mix_linattn_tm_none_kernel(tc, qc, kc, qd, st, vc_words, vc_scales, dm,
                 out=v_scales[32 * q : 32 * q + 4, :, :].bitcast(I32),
                 in_=vc_scales[:, 4 * q : 4 * q + 4, :].rearrange("a r n -> r a n").bitcast(I32),
             )
-        dm_lo = load("dm_lo", dm[lo, :])
-        v_words = sb.tile([P, 2, 2 * M], U8, name="v_words", align_bytes=64)
-        nc.sync.dma_start(out=v_words[:].bitcast(I32), in_=vc_words.rearrange("a p b -> p a b").bitcast(I32))
+        v_words = [sb.tile([P, 2 * M], U8, name="v_words%d" % a, align_bytes=64) for a in range(2)]
+        dm_early = load("dm_early", dm[lo, 0:768])
+        nc.sync.dma_start(out=v_words[0][:].bitcast(I32), in_=vc_words[0].bitcast(I32))
         st_raw = load("st_raw", st)
         qd_lo_raw = load("qd_lo_raw", qd[:, lo])
-        dm_hi_hi = load("dm_hi_hi", dm[hi, hi])
+        nc.sync.dma_start(out=v_words[1][:].bitcast(I32), in_=vc_words[1].bitcast(I32))
         qd_hi_raw = load("qd_hi_raw", qd[:, hi])
+        dm_hi_hi = load("dm_hi_hi", dm[hi, hi])
+        dm_late = load("dm_late", dm[lo, 768:1024])
 
         kc_lo, kc_hi = operand("kc_lo"), operand("kc_hi")
         qc_lo, qc_hi = operand("qc_lo"), operand("qc_hi")
@@ -120,32 +133,34 @@ def tile_mix_linattn_tm_none_kernel(tc, qc, kc, qd, st, vc_words, vc_scales, dm,
         results = [sb.tile([P, M], F32, name="result%d" % n, align_bytes=64) for n in range(8)]
         sums = {}
 
-        def value_passes(tile, h, a):
+        def value_passes(tile, h, a, start, stop):
             cols = slice((tile % 4) * TILE, (tile % 4 + 1) * TILE)
             for half in range(2):
-                if a == 0:
-                    sums[(tile, half)] = sum_pool.tile([P, HALF], F32, name="sum_bank")
+                if start:
+                    sums[(tile, half)] = psum.tile([P, HALF], F32, name="bank")
                 nc.tensor.matmul_mx(
                     out=sums[(tile, half)][:],
                     lhsT=h[1][:, cols].bitcast(FP8X4),
                     lhsT_scale=h[2][:, cols],
-                    rhs=v_words[:, a, 2 * half * HALF : 2 * (half + 1) * HALF].bitcast(FP4X4),
+                    rhs=v_words[a][:, 2 * half * HALF : 2 * (half + 1) * HALF].bitcast(FP4X4),
                     rhs_scale=v_scales[:, a, half * HALF : (half + 1) * HALF],
-                    start=(a == 0),
-                    stop=False,
+                    start=start,
+                    stop=stop,
                 )
 
-        def state_passes(tile, queries):
+        def state_passes(tile, queries, start, stop):
             cols = slice((tile % 4) * TILE, (tile % 4 + 1) * TILE)
             for half in range(2):
+                if start:
+                    sums[(tile, half)] = psum.tile([P, HALF], F32, name="bank")
                 nc.tensor.matmul_mx(
                     out=sums[(tile, half)][:],
                     lhsT=queries[1][:, cols].bitcast(FP8X4),
                     lhsT_scale=queries[2][:, cols],
                     rhs=st_half[half][1][:].bitcast(FP8X4),
                     rhs_scale=st_half[half][2][:],
-                    start=False,
-                    stop=True,
+                    start=start,
+                    stop=stop,
                 )
 
         def finish(tile, engines):
@@ -154,57 +169,78 @@ def tile_mix_linattn_tm_none_kernel(tc, qc, kc, qd, st, vc_words, vc_scales, dm,
             nc.sync.dma_start(out=out[tile * TILE : (tile + 1) * TILE, :], in_=results[tile][:])
 
         prepare_pair((kc_raw[:, :, lo], kc_lo), (kc_raw[:, :, hi], kc_hi), True)
-        prepare_pair((qc_raw[:, :, lo], qc_lo), (qc_raw[:, :, hi], qc_hi), False)
-
-        steps = [(qc_lo, dm_lo[:, :, lo], h_lo_lo, n) for n in range(4)]
-        steps = steps + [(qc_hi, dm_lo[:, :, hi], h_lo_hi, n) for n in range(4)]
-        for s, (queries, decay, h, n) in enumerate(steps):
-            weigh_tile(kc_lo, queries, decay, h, n)
-            if s > 0:
-                quantize(steps[s - 1][2], steps[s - 1][3] * TILE, (steps[s - 1][3] + 1) * TILE)
-        for tile in range(3):
-            value_passes(tile, h_lo_lo, 0)
+        prepare_pair((qc_raw[:, :, hi], qc_hi), (qc_raw[:, :, lo], qc_lo), False)
+        to_park = [(kc_hi, n) for n in range(4)] + [(kc_lo, 2), (kc_lo, 3)]
+        parked = [parked_scores("scalar", to_park[n][0], qc_hi, to_park[n][1], "parked%d" % n) for n in range(2)]
+        early = [scores(kc_lo, qc_lo, n) for n in range(4)]
+        parked = parked + [parked_scores("scalar", to_park[n][0], qc_hi, to_park[n][1], "parked%d" % n) for n in range(2, 6)]
+        early = early + [scores(kc_lo, qc_hi, n) for n in range(2)]
+        weigh(early[0], dm_early, 0, h_lo_lo, 0)
+        weigh(early[1], dm_early, 1, h_lo_lo, 1)
+        quantize_tile(h_lo_lo, 0)
+        value_passes(0, h_lo_lo, 0, True, False)
+        weigh(early[2], dm_early, 2, h_lo_lo, 2)
+        quantize_tile(h_lo_lo, 1)
+        value_passes(1, h_lo_lo, 0, True, False)
+        weigh(early[3], dm_early, 3, h_lo_lo, 3)
+        weigh(early[4], dm_early, 4, h_lo_hi, 0)
+        weigh(early[5], dm_early, 5, h_lo_hi, 1)
+        quantize(h_lo_hi, 0, 256)
 
         interleave("vector", st_raw[:, :, lo], st_half[0], 0, 256)
-        quantize(h_lo_hi, 3 * TILE, 4 * TILE)
         interleave("vector", st_raw[:, :, lo], st_half[0], 256, 512)
-        interleave("scalar", st_raw[:, :, hi], st_half[1], 0, 256)
+        interleave("vector", st_raw[:, :, hi], st_half[1], 0, 128)
+        interleave("scalar", st_raw[:, :, hi], st_half[1], 128, 256)
         interleave("scalar", st_raw[:, :, hi], st_half[1], 256, 512)
-        for half in range(2):
-            quantize(st_half[half], 0, 256)
-            quantize(st_half[half], 256, 512)
+        quantize_tile(h_lo_lo, 2)
+        value_passes(2, h_lo_lo, 0, True, False)
+        quantize(st_half[0], 0, 512)
+        quantize_tile(h_lo_lo, 3)
+        value_passes(3, h_lo_lo, 0, True, False)
+        quantize(st_half[1], 0, 512)
 
-        interleave("vector", qd_lo_raw, qd_lo, 0, 256)
+        interleave("scalar", qd_lo_raw, qd_lo, 0, 128)
+        interleave("scalar", qd_lo_raw, qd_lo, 128, 256)
+        quantize_tile(qd_lo, 0)
         interleave("vector", qd_lo_raw, qd_lo, 256, 512)
-        quantize(qd_lo, 0, 256)
+        quantize_tile(qd_lo, 1)
         quantize(qd_lo, 256, 512)
-        for tile in range(3):
-            state_passes(tile, qd_lo)
-            finish(tile, ("scalar", "scalar"))
-        value_passes(3, h_lo_lo, 0)
-        state_passes(3, qd_lo)
-
-        weigh_tile(kc_hi, qc_hi, dm_hi_hi, h_hi_hi, 0)
-        weigh_tile(kc_hi, qc_hi, dm_hi_hi, h_hi_hi, 1)
-        quantize(h_hi_hi, 0, TILE)
-        value_passes(4, h_lo_hi, 0)
-        finish(3, ("scalar", "scalar"))
-        weigh_tile(kc_hi, qc_hi, dm_hi_hi, h_hi_hi, 2)
-        quantize(h_hi_hi, TILE, 2 * TILE)
-        value_passes(5, h_lo_hi, 0)
-        weigh_tile(kc_hi, qc_hi, dm_hi_hi, h_hi_hi, 3)
-        quantize(h_hi_hi, 2 * TILE, 3 * TILE)
-        value_passes(6, h_lo_hi, 0)
-        interleave("scalar", qd_hi_raw, qd_hi, 0, 256)
+        for tile in range(4):
+            state_passes(tile, qd_lo, False, True)
+        finish(0, ("scalar", "scalar"))
+        value_passes(4, h_lo_hi, 0, True, False)
+        finish(1, ("scalar", "scalar"))
+        value_passes(5, h_lo_hi, 0, True, False)
+        interleave("vector", qd_hi_raw, qd_hi, 0, 256)
         interleave("vector", qd_hi_raw, qd_hi, 256, 512)
-        quantize(h_hi_hi, 3 * TILE, 4 * TILE)
         quantize(qd_hi, 0, 256)
         quantize(qd_hi, 256, 512)
-        for tile in range(4, 7):
-            value_passes(tile, h_hi_hi, 1)
-        for tile in range(4, 8):
-            if tile == 7:
-                value_passes(tile, h_lo_hi, 0)
-                value_passes(tile, h_hi_hi, 1)
-            state_passes(tile, qd_hi)
-            finish(tile, ("scalar", "vector"))
+        state_passes(4, qd_hi, False, False)
+        state_passes(5, qd_hi, False, False)
+        finish(2, ("scalar", "scalar"))
+        state_passes(6, qd_hi, True, False)
+        finish(3, ("scalar", "scalar"))
+
+        weigh(parked[0], dm_hi_hi, 0, h_hi_hi, 0)
+        weigh(parked[1], dm_hi_hi, 1, h_hi_hi, 1)
+        quantize_tile(h_hi_hi, 0)
+        value_passes(4, h_hi_hi, 1, False, True)
+        finish(4, ("scalar", "scalar"))
+        weigh(parked[2], dm_hi_hi, 2, h_hi_hi, 2)
+        quantize_tile(h_hi_hi, 1)
+        value_passes(5, h_hi_hi, 1, False, True)
+        state_passes(7, qd_hi, True, False)
+        finish(5, ("scalar", "scalar"))
+        weigh(parked[4], dm_late, 0, h_lo_hi, 2)
+        quantize_tile(h_hi_hi, 2)
+        value_passes(6, h_hi_hi, 1, False, False)
+        weigh(parked[5], dm_late, 1, h_lo_hi, 3)
+        quantize_tile(h_lo_hi, 2)
+        value_passes(6, h_lo_hi, 0, False, True)
+        weigh(parked[3], dm_hi_hi, 3, h_hi_hi, 3)
+        quantize_tile(h_lo_hi, 3)
+        value_passes(7, h_lo_hi, 0, False, False)
+        quantize_tile(h_hi_hi, 3)
+        value_passes(7, h_hi_hi, 1, False, True)
+        finish(6, ("scalar", "vector"))
+        finish(7, ("scalar", "vector"))

@@ -13,12 +13,14 @@ U32 = mybir.dt.uint32
 U8 = mybir.dt.uint8
 FP8X4 = mybir.dt.float8_e4m3fn_x4
 FP4X4 = mybir.dt.float4_e2m1fn_x4
-MULT = mybir.AluOpType.mult
 
 P = 128
 PACK = 4
 HALF = 512
 TILE = 128
+QUADRANT = 32
+BANKS = 8
+EARLY_QUERIES = 768
 
 
 def tile_mix_linattn_tm_none_kernel(tc, qc, kc, qd, st, vc_words, vc_scales, dm, out):
@@ -26,19 +28,22 @@ def tile_mix_linattn_tm_none_kernel(tc, qc, kc, qd, st, vc_words, vc_scales, dm,
 
     with ExitStack() as ctx:
         sb = ctx.enter_context(tc.tile_pool(name="sb", bufs=1))
-        psum = ctx.enter_context(tc.psum_pool(name="psum", bufs=8))
+        psum = ctx.enter_context(tc.psum_pool(name="psum", bufs=BANKS))
         ctx.enter_context(tc.manual_schedule())
 
         def load(name, rows):
-            raw = sb.tile([P, PACK, rows.shape[1]], F32, name=name, align_bytes=64)
-            nc.sync.dma_start(out=raw[:], in_=rows.rearrange("(p e) w -> p e w", e=PACK))
+            raw = sb.tile([rows.shape[0] // PACK, PACK, rows.shape[1]], F32, name=name, align_bytes=64)
+            nc.sync.dma_start(out=raw[:], in_=rows.rearrange("(p i) w -> p i w", i=PACK))
             return raw
 
         def operand(name):
             staged = sb.tile([P, HALF * PACK], BF16, name=name + "_bf", align_bytes=64)
             codes = sb.tile([P, HALF], U32, name=name + "_codes", align_bytes=64)
             scales = sb.tile([P, HALF], U8, name=name + "_scales", align_bytes=64)
-            return staged, codes, scales
+            return {"staged": staged, "codes": codes, "scales": scales}
+
+        def tile_cols(n):
+            return slice(n * TILE, (n + 1) * TILE)
 
         def copy_on(engine, dst, src):
             if engine == "vector":
@@ -47,19 +52,24 @@ def tile_mix_linattn_tm_none_kernel(tc, qc, kc, qd, st, vc_words, vc_scales, dm,
                 nc.scalar.copy(out=dst, in_=src)
 
         def interleave(engine, raw, op, c0, c1):
-            dst = op[0][:, PACK * c0 : PACK * c1].rearrange("p (c u e) -> p c e u", u=2, e=PACK)
-            src = raw[:, :, c0:c1].rearrange("p e (c u) -> p c e u", u=2)
+            dst = op["staged"][:, PACK * c0 : PACK * c1].rearrange("p (c u i) -> p c i u", u=2, i=PACK)
+            src = raw[:, :, c0:c1].rearrange("p i (c u) -> p c i u", u=2)
             copy_on(engine, dst, src)
 
         def interleave_keys(engine, raw, op, i0):
-            dst = op[0][:].rearrange("p (i m e) -> p m e i", i=PACK, e=PACK)[:, :, :, i0 : i0 + 2]
+            dst = op["staged"][:].rearrange("p (i m e) -> p m e i", i=PACK, e=PACK)[:, :, :, i0 : i0 + 2]
             src = raw.rearrange("p e (m i) -> p m e i", i=PACK)[:, :, :, i0 : i0 + 2]
             copy_on(engine, dst, src)
 
         def quantize(op, c0, c1):
             nc.vector.quantize_mx(
-                out=op[1][:, c0:c1].bitcast(FP8X4), scales=op[2][:, c0:c1], in_=op[0][:, PACK * c0 : PACK * c1]
+                out=op["codes"][:, c0:c1].bitcast(FP8X4),
+                scales=op["scales"][:, c0:c1],
+                in_=op["staged"][:, PACK * c0 : PACK * c1],
             )
+
+        def quantize_tile(op, n):
+            quantize(op, n * TILE, (n + 1) * TILE)
 
         def prepare_pair(on_vector, on_scalar, is_keys):
             for engine, (raw, op) in (("vector", on_vector), ("scalar", on_scalar)):
@@ -67,180 +77,187 @@ def tile_mix_linattn_tm_none_kernel(tc, qc, kc, qd, st, vc_words, vc_scales, dm,
                     if is_keys:
                         interleave_keys(engine, raw, op, 2 * part)
                     else:
-                        interleave(engine, raw, op, 256 * part, 256 * (part + 1))
-            for (raw, op) in (on_vector, on_scalar):
-                quantize(op, 0, 256)
-                quantize(op, 256, 512)
+                        interleave(engine, raw, op, 2 * TILE * part, 2 * TILE * (part + 1))
+            for raw, op in (on_vector, on_scalar):
+                quantize(op, 0, 2 * TILE)
+                quantize(op, 2 * TILE, HALF)
 
         def scores(keys, queries, n):
-            cols = slice(n * TILE, (n + 1) * TILE)
             bank = psum.tile([P, HALF], F32, name="bank")
             for i in range(PACK):
-                key_cols = slice(i * TILE, (i + 1) * TILE)
                 nc.tensor.matmul_mx(
-                    out=bank[:, key_cols],
-                    lhsT=keys[1][:, key_cols].bitcast(FP8X4),
-                    lhsT_scale=keys[2][:, key_cols],
-                    rhs=queries[1][:, cols].bitcast(FP8X4),
-                    rhs_scale=queries[2][:, cols],
+                    out=bank[:, tile_cols(i)],
+                    lhsT=keys["codes"][:, tile_cols(i)].bitcast(FP8X4),
+                    lhsT_scale=keys["scales"][:, tile_cols(i)],
+                    rhs=queries["codes"][:, tile_cols(n)].bitcast(FP8X4),
+                    rhs_scale=queries["scales"][:, tile_cols(n)],
                     start=True,
                     stop=True,
                 )
             return bank
 
-        def parked_scores(engine, keys, queries, n, name):
+        def parked_scores(keys, queries, n, name, parts):
             bank = scores(keys, queries, n)
-            parked = sb.tile([P, HALF], F32, name=name, align_bytes=64)
-            copy_on(engine, parked[:], bank[:])
+            parked = sb.tile([parts, HALF], F32, name=name, align_bytes=64)
+            nc.scalar.copy(out=parked[:], in_=bank[0:parts, :])
             return parked
 
         def weigh(raw_scores, decay, d, h, n):
+            parts = decay.shape[0]
             nc.vector.tensor_tensor(
-                out=h[0][:, PACK * n * TILE : PACK * (n + 1) * TILE].rearrange("p (c u i) -> p c i u", u=2, i=PACK),
-                in0=raw_scores[:].rearrange("p (i c u) -> p c i u", u=2, i=PACK),
-                in1=decay[:, :, d * TILE : (d + 1) * TILE].rearrange("p i (c u) -> p c i u", u=2),
-                op=MULT,
+                out=h["staged"][0:parts, PACK * n * TILE : PACK * (n + 1) * TILE].rearrange(
+                    "p (c u i) -> p c i u", u=2, i=PACK
+                ),
+                in0=raw_scores[0:parts, :].rearrange("p (i c u) -> p c i u", u=2, i=PACK),
+                in1=decay[:, :, tile_cols(d)].rearrange("p i (c u) -> p c i u", u=2),
+                op=mybir.AluOpType.mult,
             )
-
-        def quantize_tile(op, n):
-            quantize(op, n * TILE, (n + 1) * TILE)
 
         lo, hi = slice(0, HALF), slice(HALF, T)
         v_scales = sb.tile([P, 2, M], U8, name="v_scales", align_bytes=64)
         nc.vector.memset(v_scales[:].rearrange("p a n -> p (a n)").bitcast(I32), 0)
         kc_raw = load("kc_raw", kc)
         qc_raw = load("qc_raw", qc)
-        for q in range(4):
+        for q in range(P // QUADRANT):
             nc.scalar.dma_start(
-                out=v_scales[32 * q : 32 * q + 4, :, :].bitcast(I32),
+                out=v_scales[QUADRANT * q : QUADRANT * q + 4, :, :].bitcast(I32),
                 in_=vc_scales[:, 4 * q : 4 * q + 4, :].rearrange("a r n -> r a n").bitcast(I32),
             )
         v_words = [sb.tile([P, 2 * M], U8, name="v_words%d" % a, align_bytes=64) for a in range(2)]
-        dm_early = load("dm_early", dm[lo, 0:768])
+        dm_corner_lo = load("dm_corner_lo", dm[0:TILE, 0:TILE])
+        dm_early = load("dm_early", dm[lo, TILE:EARLY_QUERIES])
         nc.sync.dma_start(out=v_words[0][:].bitcast(I32), in_=vc_words[0].bitcast(I32))
         st_raw = load("st_raw", st)
         qd_lo_raw = load("qd_lo_raw", qd[:, lo])
         nc.sync.dma_start(out=v_words[1][:].bitcast(I32), in_=vc_words[1].bitcast(I32))
         qd_hi_raw = load("qd_hi_raw", qd[:, hi])
-        dm_hi_hi = load("dm_hi_hi", dm[hi, hi])
-        dm_late = load("dm_late", dm[lo, 768:1024])
+        dm_corner_hi = load("dm_corner_hi", dm[HALF : HALF + TILE, HALF : HALF + TILE])
+        dm_hi = load("dm_hi", dm[hi, HALF + TILE : T])
+        dm_late = load("dm_late", dm[lo, EARLY_QUERIES:T])
 
         kc_lo, kc_hi = operand("kc_lo"), operand("kc_hi")
         qc_lo, qc_hi = operand("qc_lo"), operand("qc_hi")
         qd_lo, qd_hi = operand("qd_lo"), operand("qd_hi")
         st_half = [operand("st_lo"), operand("st_hi")]
         h_lo_hi, h_hi_hi, h_lo_lo = operand("h_lo_hi"), operand("h_hi_hi"), operand("h_lo_lo")
-        results = [sb.tile([P, M], F32, name="result%d" % n, align_bytes=64) for n in range(8)]
+        results = [sb.tile([P, M], F32, name="result%d" % n, align_bytes=64) for n in range(T // TILE)]
         sums = {}
+        for h in (h_lo_lo, h_hi_hi):
+            nc.vector.memset(h["staged"][:, 0 : PACK * TILE], 0.0)
 
-        def value_passes(tile, h, a, start, stop):
-            cols = slice((tile % 4) * TILE, (tile % 4 + 1) * TILE)
+        def sum_passes(tile, left, right, start, stop):
+            cols = tile_cols(tile % (HALF // TILE))
             for half in range(2):
                 if start:
                     sums[(tile, half)] = psum.tile([P, HALF], F32, name="bank")
+                codes, scales = right(half)
                 nc.tensor.matmul_mx(
                     out=sums[(tile, half)][:],
-                    lhsT=h[1][:, cols].bitcast(FP8X4),
-                    lhsT_scale=h[2][:, cols],
-                    rhs=v_words[a][:, 2 * half * HALF : 2 * (half + 1) * HALF].bitcast(FP4X4),
-                    rhs_scale=v_scales[:, a, half * HALF : (half + 1) * HALF],
+                    lhsT=left["codes"][:, cols].bitcast(FP8X4),
+                    lhsT_scale=left["scales"][:, cols],
+                    rhs=codes,
+                    rhs_scale=scales,
                     start=start,
                     stop=stop,
                 )
 
-        def state_passes(tile, queries, start, stop):
-            cols = slice((tile % 4) * TILE, (tile % 4 + 1) * TILE)
-            for half in range(2):
-                if start:
-                    sums[(tile, half)] = psum.tile([P, HALF], F32, name="bank")
-                nc.tensor.matmul_mx(
-                    out=sums[(tile, half)][:],
-                    lhsT=queries[1][:, cols].bitcast(FP8X4),
-                    lhsT_scale=queries[2][:, cols],
-                    rhs=st_half[half][1][:].bitcast(FP8X4),
-                    rhs_scale=st_half[half][2][:],
-                    start=start,
-                    stop=stop,
-                )
+        def value_passes(tile, h, a, start=False, stop=False):
+            sum_passes(
+                tile,
+                h,
+                lambda half: (
+                    v_words[a][:, 2 * half * HALF : 2 * (half + 1) * HALF].bitcast(FP4X4),
+                    v_scales[:, a, half * HALF : (half + 1) * HALF],
+                ),
+                start,
+                stop,
+            )
 
-        def finish(tile, engines):
-            for half in range(2):
-                copy_on(engines[half], results[tile][:, half * HALF : (half + 1) * HALF], sums[(tile, half)][:])
-            nc.sync.dma_start(out=out[tile * TILE : (tile + 1) * TILE, :], in_=results[tile][:])
+        def state_passes(tile, queries, start=False, stop=False):
+            sum_passes(
+                tile,
+                queries,
+                lambda half: (st_half[half]["codes"][:].bitcast(FP8X4), st_half[half]["scales"][:]),
+                start,
+                stop,
+            )
+
+        def finish(tile, second_engine):
+            for half, engine in enumerate(("scalar", second_engine)):
+                copy_on(engine, results[tile][:, half * HALF : (half + 1) * HALF], sums[(tile, half)][:])
+            nc.sync.dma_start(out=out[tile_cols(tile), :], in_=results[tile][:])
 
         prepare_pair((kc_raw[:, :, lo], kc_lo), (kc_raw[:, :, hi], kc_hi), True)
         prepare_pair((qc_raw[:, :, hi], qc_hi), (qc_raw[:, :, lo], qc_lo), False)
-        to_park = [(kc_hi, n) for n in range(4)] + [(kc_lo, 2), (kc_lo, 3)]
-        parked = [parked_scores("scalar", to_park[n][0], qc_hi, to_park[n][1], "parked%d" % n) for n in range(2)]
+        parked_hi = [parked_scores(kc_hi, qc_hi, n, "parked_hi%d" % n, QUADRANT if n == 0 else P) for n in (0, 1)]
         early = [scores(kc_lo, qc_lo, n) for n in range(4)]
-        parked = parked + [parked_scores("scalar", to_park[n][0], qc_hi, to_park[n][1], "parked%d" % n) for n in range(2, 6)]
-        early = early + [scores(kc_lo, qc_hi, n) for n in range(2)]
-        weigh(early[0], dm_early, 0, h_lo_lo, 0)
-        weigh(early[1], dm_early, 1, h_lo_lo, 1)
+        parked_hi = parked_hi + [parked_scores(kc_hi, qc_hi, n, "parked_hi%d" % n, P) for n in (2, 3)]
+        parked_late = [parked_scores(kc_lo, qc_hi, n, "parked_late%d" % n, P) for n in (2, 3)]
+        early = early + [scores(kc_lo, qc_hi, n) for n in (0, 1)]
+
+        weigh(early[0], dm_corner_lo, 0, h_lo_lo, 0)
+        weigh(early[1], dm_early, 0, h_lo_lo, 1)
         quantize_tile(h_lo_lo, 0)
-        value_passes(0, h_lo_lo, 0, True, False)
-        weigh(early[2], dm_early, 2, h_lo_lo, 2)
+        value_passes(0, h_lo_lo, 0, start=True)
+        weigh(early[2], dm_early, 1, h_lo_lo, 2)
         quantize_tile(h_lo_lo, 1)
-        value_passes(1, h_lo_lo, 0, True, False)
-        weigh(early[3], dm_early, 3, h_lo_lo, 3)
-        weigh(early[4], dm_early, 4, h_lo_hi, 0)
-        weigh(early[5], dm_early, 5, h_lo_hi, 1)
-        quantize(h_lo_hi, 0, 256)
+        value_passes(1, h_lo_lo, 0, start=True)
+        weigh(early[3], dm_early, 2, h_lo_lo, 3)
+        weigh(early[4], dm_early, 3, h_lo_hi, 0)
+        weigh(early[5], dm_early, 4, h_lo_hi, 1)
+        quantize(h_lo_hi, 0, 2 * TILE)
 
-        interleave("vector", st_raw[:, :, lo], st_half[0], 0, 256)
-        interleave("vector", st_raw[:, :, lo], st_half[0], 256, 512)
-        interleave("vector", st_raw[:, :, hi], st_half[1], 0, 128)
-        interleave("scalar", st_raw[:, :, hi], st_half[1], 128, 256)
-        interleave("scalar", st_raw[:, :, hi], st_half[1], 256, 512)
-        quantize_tile(h_lo_lo, 2)
-        value_passes(2, h_lo_lo, 0, True, False)
-        quantize(st_half[0], 0, 512)
-        quantize_tile(h_lo_lo, 3)
-        value_passes(3, h_lo_lo, 0, True, False)
-        quantize(st_half[1], 0, 512)
+        interleave("vector", st_raw[:, :, lo], st_half[0], 0, 2 * TILE)
+        interleave("vector", st_raw[:, :, lo], st_half[0], 2 * TILE, HALF)
+        interleave("vector", st_raw[:, :, hi], st_half[1], 0, TILE)
+        interleave("scalar", st_raw[:, :, hi], st_half[1], TILE, 2 * TILE)
+        interleave("scalar", st_raw[:, :, hi], st_half[1], 2 * TILE, HALF)
+        for half in range(2):
+            quantize_tile(h_lo_lo, 2 + half)
+            value_passes(2 + half, h_lo_lo, 0, start=True)
+            quantize(st_half[half], 0, HALF)
 
-        interleave("scalar", qd_lo_raw, qd_lo, 0, 128)
-        interleave("scalar", qd_lo_raw, qd_lo, 128, 256)
+        interleave("scalar", qd_lo_raw, qd_lo, 0, TILE)
+        interleave("scalar", qd_lo_raw, qd_lo, TILE, 2 * TILE)
         quantize_tile(qd_lo, 0)
-        interleave("vector", qd_lo_raw, qd_lo, 256, 512)
+        interleave("vector", qd_lo_raw, qd_lo, 2 * TILE, HALF)
         quantize_tile(qd_lo, 1)
-        quantize(qd_lo, 256, 512)
+        quantize(qd_lo, 2 * TILE, HALF)
         for tile in range(4):
-            state_passes(tile, qd_lo, False, True)
-        finish(0, ("scalar", "scalar"))
-        value_passes(4, h_lo_hi, 0, True, False)
-        finish(1, ("scalar", "scalar"))
-        value_passes(5, h_lo_hi, 0, True, False)
-        interleave("vector", qd_hi_raw, qd_hi, 0, 256)
-        interleave("vector", qd_hi_raw, qd_hi, 256, 512)
-        quantize(qd_hi, 0, 256)
-        quantize(qd_hi, 256, 512)
-        state_passes(4, qd_hi, False, False)
-        state_passes(5, qd_hi, False, False)
-        finish(2, ("scalar", "scalar"))
-        state_passes(6, qd_hi, True, False)
-        finish(3, ("scalar", "scalar"))
+            state_passes(tile, qd_lo, stop=True)
+        for tile in (0, 1):
+            finish(tile, "scalar")
+            value_passes(4 + tile, h_lo_hi, 0, start=True)
+        interleave("vector", qd_hi_raw, qd_hi, 0, 2 * TILE)
+        interleave("vector", qd_hi_raw, qd_hi, 2 * TILE, HALF)
+        quantize(qd_hi, 0, 2 * TILE)
+        quantize(qd_hi, 2 * TILE, HALF)
+        state_passes(4, qd_hi)
+        state_passes(5, qd_hi)
+        finish(2, "scalar")
+        state_passes(6, qd_hi, start=True)
+        finish(3, "scalar")
 
-        weigh(parked[0], dm_hi_hi, 0, h_hi_hi, 0)
-        weigh(parked[1], dm_hi_hi, 1, h_hi_hi, 1)
+        weigh(parked_hi[0], dm_corner_hi, 0, h_hi_hi, 0)
+        weigh(parked_hi[1], dm_hi, 0, h_hi_hi, 1)
         quantize_tile(h_hi_hi, 0)
-        value_passes(4, h_hi_hi, 1, False, True)
-        finish(4, ("scalar", "scalar"))
-        weigh(parked[2], dm_hi_hi, 2, h_hi_hi, 2)
+        value_passes(4, h_hi_hi, 1, stop=True)
+        finish(4, "scalar")
+        weigh(parked_hi[2], dm_hi, 1, h_hi_hi, 2)
         quantize_tile(h_hi_hi, 1)
-        value_passes(5, h_hi_hi, 1, False, True)
-        state_passes(7, qd_hi, True, False)
-        finish(5, ("scalar", "scalar"))
-        weigh(parked[4], dm_late, 0, h_lo_hi, 2)
+        value_passes(5, h_hi_hi, 1, stop=True)
+        state_passes(7, qd_hi, start=True)
+        finish(5, "scalar")
+        weigh(parked_late[0], dm_late, 0, h_lo_hi, 2)
         quantize_tile(h_hi_hi, 2)
-        value_passes(6, h_hi_hi, 1, False, False)
-        weigh(parked[5], dm_late, 1, h_lo_hi, 3)
+        value_passes(6, h_hi_hi, 1)
+        weigh(parked_late[1], dm_late, 1, h_lo_hi, 3)
         quantize_tile(h_lo_hi, 2)
-        value_passes(6, h_lo_hi, 0, False, True)
-        weigh(parked[3], dm_hi_hi, 3, h_hi_hi, 3)
+        value_passes(6, h_lo_hi, 0, stop=True)
+        weigh(parked_hi[3], dm_hi, 2, h_hi_hi, 3)
         quantize_tile(h_lo_hi, 3)
-        value_passes(7, h_lo_hi, 0, False, False)
+        value_passes(7, h_lo_hi, 0)
         quantize_tile(h_hi_hi, 3)
-        value_passes(7, h_hi_hi, 1, False, True)
-        finish(6, ("scalar", "vector"))
-        finish(7, ("scalar", "vector"))
+        value_passes(7, h_hi_hi, 1, stop=True)
+        finish(6, "vector")
+        finish(7, "vector")

from contextlib import ExitStack

import concourse.mybir as mybir

K, M, T = 512, 1024, 1024
FLOPS = 2 * K * T * T // 2 + 2 * T * T * M // 2 + 2 * K * T * M
BYTES = 4 * (4 * K * T + T * T // 2 + T * M) + T * M // 2 + T * M // 32

F32 = mybir.dt.float32
BF16 = mybir.dt.bfloat16
I32 = mybir.dt.int32
U32 = mybir.dt.uint32
U8 = mybir.dt.uint8
FP8X4 = mybir.dt.float8_e4m3fn_x4
FP4X4 = mybir.dt.float4_e2m1fn_x4

P = 128
PACK = 4
HALF = 512
TILE = 128
QUADRANT = 32
BANKS = 8
EARLY_QUERIES = 768


def tile_mix_linattn_tm_none_kernel(tc, qc, kc, qd, st, vc_words, vc_scales, dm, out):
    nc = tc.nc

    with ExitStack() as ctx:
        sb = ctx.enter_context(tc.tile_pool(name="sb", bufs=1))
        psum = ctx.enter_context(tc.psum_pool(name="psum", bufs=BANKS))
        ctx.enter_context(tc.manual_schedule())

        def load(name, rows):
            raw = sb.tile([rows.shape[0] // PACK, PACK, rows.shape[1]], F32, name=name, align_bytes=64)
            nc.sync.dma_start(out=raw[:], in_=rows.rearrange("(p i) w -> p i w", i=PACK))
            return raw

        def operand(name):
            staged = sb.tile([P, HALF * PACK], BF16, name=name + "_bf", align_bytes=64)
            codes = sb.tile([P, HALF], U32, name=name + "_codes", align_bytes=64)
            scales = sb.tile([P, HALF], U8, name=name + "_scales", align_bytes=64)
            return {"staged": staged, "codes": codes, "scales": scales}

        def tile_cols(n):
            return slice(n * TILE, (n + 1) * TILE)

        def copy_on(engine, dst, src):
            if engine == "vector":
                nc.vector.tensor_copy(out=dst, in_=src)
            else:
                nc.scalar.copy(out=dst, in_=src)

        def interleave(engine, raw, op, c0, c1):
            dst = op["staged"][:, PACK * c0 : PACK * c1].rearrange("p (c u i) -> p c i u", u=2, i=PACK)
            src = raw[:, :, c0:c1].rearrange("p i (c u) -> p c i u", u=2)
            copy_on(engine, dst, src)

        def interleave_keys(engine, raw, op, i0):
            dst = op["staged"][:].rearrange("p (i m e) -> p m e i", i=PACK, e=PACK)[:, :, :, i0 : i0 + 2]
            src = raw.rearrange("p e (m i) -> p m e i", i=PACK)[:, :, :, i0 : i0 + 2]
            copy_on(engine, dst, src)

        def quantize(op, c0, c1):
            nc.vector.quantize_mx(
                out=op["codes"][:, c0:c1].bitcast(FP8X4),
                scales=op["scales"][:, c0:c1],
                in_=op["staged"][:, PACK * c0 : PACK * c1],
            )

        def quantize_tile(op, n):
            quantize(op, n * TILE, (n + 1) * TILE)

        def prepare_pair(on_vector, on_scalar, is_keys):
            for engine, (raw, op) in (("vector", on_vector), ("scalar", on_scalar)):
                for part in range(2):
                    if is_keys:
                        interleave_keys(engine, raw, op, 2 * part)
                    else:
                        interleave(engine, raw, op, 2 * TILE * part, 2 * TILE * (part + 1))
            for raw, op in (on_vector, on_scalar):
                quantize(op, 0, 2 * TILE)
                quantize(op, 2 * TILE, HALF)

        def scores(keys, queries, n):
            bank = psum.tile([P, HALF], F32, name="bank")
            for i in range(PACK):
                nc.tensor.matmul_mx(
                    out=bank[:, tile_cols(i)],
                    lhsT=keys["codes"][:, tile_cols(i)].bitcast(FP8X4),
                    lhsT_scale=keys["scales"][:, tile_cols(i)],
                    rhs=queries["codes"][:, tile_cols(n)].bitcast(FP8X4),
                    rhs_scale=queries["scales"][:, tile_cols(n)],
                    start=True,
                    stop=True,
                )
            return bank

        def parked_scores(keys, queries, n, name, parts):
            bank = scores(keys, queries, n)
            parked = sb.tile([parts, HALF], F32, name=name, align_bytes=64)
            nc.scalar.copy(out=parked[:], in_=bank[0:parts, :])
            return parked

        def weigh(raw_scores, decay, d, h, n):
            parts = decay.shape[0]
            nc.vector.tensor_tensor(
                out=h["staged"][0:parts, PACK * n * TILE : PACK * (n + 1) * TILE].rearrange(
                    "p (c u i) -> p c i u", u=2, i=PACK
                ),
                in0=raw_scores[0:parts, :].rearrange("p (i c u) -> p c i u", u=2, i=PACK),
                in1=decay[:, :, tile_cols(d)].rearrange("p i (c u) -> p c i u", u=2),
                op=mybir.AluOpType.mult,
            )

        lo, hi = slice(0, HALF), slice(HALF, T)
        v_scales = sb.tile([P, 2, M], U8, name="v_scales", align_bytes=64)
        nc.vector.memset(v_scales[:].rearrange("p a n -> p (a n)").bitcast(I32), 0)
        kc_raw = load("kc_raw", kc)
        qc_raw = load("qc_raw", qc)
        for q in range(P // QUADRANT):
            nc.scalar.dma_start(
                out=v_scales[QUADRANT * q : QUADRANT * q + 4, :, :].bitcast(I32),
                in_=vc_scales[:, 4 * q : 4 * q + 4, :].rearrange("a r n -> r a n").bitcast(I32),
            )
        v_words = [sb.tile([P, 2 * M], U8, name="v_words%d" % a, align_bytes=64) for a in range(2)]
        dm_corner_lo = load("dm_corner_lo", dm[0:TILE, 0:TILE])
        dm_early = load("dm_early", dm[lo, TILE:EARLY_QUERIES])
        nc.sync.dma_start(out=v_words[0][:].bitcast(I32), in_=vc_words[0].bitcast(I32))
        st_raw = load("st_raw", st)
        qd_lo_raw = load("qd_lo_raw", qd[:, lo])
        nc.sync.dma_start(out=v_words[1][:].bitcast(I32), in_=vc_words[1].bitcast(I32))
        qd_hi_raw = load("qd_hi_raw", qd[:, hi])
        dm_corner_hi = load("dm_corner_hi", dm[HALF : HALF + TILE, HALF : HALF + TILE])
        dm_hi = load("dm_hi", dm[hi, HALF + TILE : T])
        dm_late = load("dm_late", dm[lo, EARLY_QUERIES:T])

        kc_lo, kc_hi = operand("kc_lo"), operand("kc_hi")
        qc_lo, qc_hi = operand("qc_lo"), operand("qc_hi")
        qd_lo, qd_hi = operand("qd_lo"), operand("qd_hi")
        st_half = [operand("st_lo"), operand("st_hi")]
        h_lo_hi, h_hi_hi, h_lo_lo = operand("h_lo_hi"), operand("h_hi_hi"), operand("h_lo_lo")
        results = [sb.tile([P, M], F32, name="result%d" % n, align_bytes=64) for n in range(T // TILE)]
        sums = {}
        for h in (h_lo_lo, h_hi_hi):
            nc.vector.memset(h["staged"][:, 0 : PACK * TILE], 0.0)

        def sum_passes(tile, left, right, start, stop):
            cols = tile_cols(tile % (HALF // TILE))
            for half in range(2):
                if start:
                    sums[(tile, half)] = psum.tile([P, HALF], F32, name="bank")
                codes, scales = right(half)
                nc.tensor.matmul_mx(
                    out=sums[(tile, half)][:],
                    lhsT=left["codes"][:, cols].bitcast(FP8X4),
                    lhsT_scale=left["scales"][:, cols],
                    rhs=codes,
                    rhs_scale=scales,
                    start=start,
                    stop=stop,
                )

        def value_passes(tile, h, a, start=False, stop=False):
            sum_passes(
                tile,
                h,
                lambda half: (
                    v_words[a][:, 2 * half * HALF : 2 * (half + 1) * HALF].bitcast(FP4X4),
                    v_scales[:, a, half * HALF : (half + 1) * HALF],
                ),
                start,
                stop,
            )

        def state_passes(tile, queries, start=False, stop=False):
            sum_passes(
                tile,
                queries,
                lambda half: (st_half[half]["codes"][:].bitcast(FP8X4), st_half[half]["scales"][:]),
                start,
                stop,
            )

        def finish(tile, second_engine):
            for half, engine in enumerate(("scalar", second_engine)):
                copy_on(engine, results[tile][:, half * HALF : (half + 1) * HALF], sums[(tile, half)][:])
            nc.sync.dma_start(out=out[tile_cols(tile), :], in_=results[tile][:])

        prepare_pair((kc_raw[:, :, lo], kc_lo), (kc_raw[:, :, hi], kc_hi), True)
        prepare_pair((qc_raw[:, :, hi], qc_hi), (qc_raw[:, :, lo], qc_lo), False)
        parked_hi = [parked_scores(kc_hi, qc_hi, n, "parked_hi%d" % n, QUADRANT if n == 0 else P) for n in (0, 1)]
        early = [scores(kc_lo, qc_lo, n) for n in range(4)]
        parked_hi = parked_hi + [parked_scores(kc_hi, qc_hi, n, "parked_hi%d" % n, P) for n in (2, 3)]
        parked_late = [parked_scores(kc_lo, qc_hi, n, "parked_late%d" % n, P) for n in (2, 3)]
        early = early + [scores(kc_lo, qc_hi, n) for n in (0, 1)]

        weigh(early[0], dm_corner_lo, 0, h_lo_lo, 0)
        weigh(early[1], dm_early, 0, h_lo_lo, 1)
        quantize_tile(h_lo_lo, 0)
        value_passes(0, h_lo_lo, 0, start=True)
        weigh(early[2], dm_early, 1, h_lo_lo, 2)
        quantize_tile(h_lo_lo, 1)
        value_passes(1, h_lo_lo, 0, start=True)
        weigh(early[3], dm_early, 2, h_lo_lo, 3)
        weigh(early[4], dm_early, 3, h_lo_hi, 0)
        weigh(early[5], dm_early, 4, h_lo_hi, 1)
        quantize(h_lo_hi, 0, 2 * TILE)

        interleave("vector", st_raw[:, :, lo], st_half[0], 0, 2 * TILE)
        interleave("vector", st_raw[:, :, lo], st_half[0], 2 * TILE, HALF)
        interleave("vector", st_raw[:, :, hi], st_half[1], 0, TILE)
        interleave("scalar", st_raw[:, :, hi], st_half[1], TILE, 2 * TILE)
        interleave("scalar", st_raw[:, :, hi], st_half[1], 2 * TILE, HALF)
        for half in range(2):
            quantize_tile(h_lo_lo, 2 + half)
            value_passes(2 + half, h_lo_lo, 0, start=True)
            quantize(st_half[half], 0, HALF)

        interleave("scalar", qd_lo_raw, qd_lo, 0, TILE)
        interleave("scalar", qd_lo_raw, qd_lo, TILE, 2 * TILE)
        quantize_tile(qd_lo, 0)
        interleave("vector", qd_lo_raw, qd_lo, 2 * TILE, HALF)
        quantize_tile(qd_lo, 1)
        quantize(qd_lo, 2 * TILE, HALF)
        for tile in range(4):
            state_passes(tile, qd_lo, stop=True)
        for tile in (0, 1):
            finish(tile, "scalar")
            value_passes(4 + tile, h_lo_hi, 0, start=True)
        interleave("vector", qd_hi_raw, qd_hi, 0, 2 * TILE)
        interleave("vector", qd_hi_raw, qd_hi, 2 * TILE, HALF)
        quantize(qd_hi, 0, 2 * TILE)
        quantize(qd_hi, 2 * TILE, HALF)
        state_passes(4, qd_hi)
        state_passes(5, qd_hi)
        finish(2, "scalar")
        state_passes(6, qd_hi, start=True)
        finish(3, "scalar")

        weigh(parked_hi[0], dm_corner_hi, 0, h_hi_hi, 0)
        weigh(parked_hi[1], dm_hi, 0, h_hi_hi, 1)
        quantize_tile(h_hi_hi, 0)
        value_passes(4, h_hi_hi, 1, stop=True)
        finish(4, "scalar")
        weigh(parked_hi[2], dm_hi, 1, h_hi_hi, 2)
        quantize_tile(h_hi_hi, 1)
        value_passes(5, h_hi_hi, 1, stop=True)
        state_passes(7, qd_hi, start=True)
        finish(5, "scalar")
        weigh(parked_late[0], dm_late, 0, h_lo_hi, 2)
        quantize_tile(h_hi_hi, 2)
        value_passes(6, h_hi_hi, 1)
        weigh(parked_late[1], dm_late, 1, h_lo_hi, 3)
        quantize_tile(h_lo_hi, 2)
        value_passes(6, h_lo_hi, 0, stop=True)
        weigh(parked_hi[3], dm_hi, 2, h_hi_hi, 3)
        quantize_tile(h_lo_hi, 3)
        value_passes(7, h_lo_hi, 0)
        quantize_tile(h_hi_hi, 3)
        value_passes(7, h_hi_hi, 1, stop=True)
        finish(6, "vector")
        finish(7, "vector")
